import numpy as np
import ml_dtypes


def mxq(x, axis, fmt="e4m3"):
    dtype, down = {"e4m3": (ml_dtypes.float8_e4m3fn, 7), "e5m2": (ml_dtypes.float8_e5m2, 14)}[fmt]
    v = np.moveaxis(np.asarray(x, np.float32).astype(ml_dtypes.bfloat16).astype(np.float64), axis, -1)
    blocks = v.reshape(v.shape[:-1] + (-1, 32))
    amax = np.abs(blocks).max(-1, keepdims=True)
    byte = np.maximum(np.where(amax > 0, np.frexp(amax)[1] - 1 + 127, 0) - down, 1)
    scale = np.exp2(byte - 127.0)
    codes = (blocks / scale).astype(np.float32).astype(dtype).astype(np.float64)
    return np.moveaxis((codes * scale).reshape(v.shape), -1, axis)


WIDE = False


def mx_kscale(k):
    if not WIDE:
        return np.ones(k)
    levels = np.array([10, -10, 5, -5, 0])
    if k % 512:
        return np.exp2(np.random.permutation(np.resize(levels, k // 32))).repeat(32)
    a = np.empty((k // 512, 16))
    for p in range(k // 512):
        a[p, :8] = np.random.permutation(np.resize(levels, 8))
        for g in range(8):
            far = levels[np.abs(levels - a[p, g]) >= 10]
            a[p, g + 8] = far[np.random.randint(len(far))]
    return np.exp2(a.ravel()).repeat(32)


def f64(x):
    return np.asarray(x).astype(np.float64)


def striped8(idx):
    return np.asarray(idx).reshape(8, -1, 16).transpose(0, 2, 1).reshape(128, -1).astype(np.uint16)


def unstriped8(offs):
    return offs.reshape(8, 16, -1).transpose(0, 2, 1).reshape(8, -1).astype(np.int64)


def pick8(x, idx, run):
    r = np.arange(len(x))
    return x[r[:, None], idx[r % (8 * run) // run]]


E2M1 = np.array([0.0, 0.5, 1.0, 1.5, 2.0, 3.0, 4.0, 6.0, -0.0, -0.5, -1.0, -1.5, -2.0, -3.0, -4.0, -6.0])


def pack_weight(w, fmt):
    k, n = w.shape
    w = f64(np.asarray(w, np.float32).astype(ml_dtypes.bfloat16)).reshape(k // 32, 32, n)
    amax = np.abs(w).max(1)
    if fmt == "e4m3":
        byte = np.frexp(amax)[1] - 1 + 127 - 7
    else:
        mant, ex = np.frexp(amax / 6.0)
        byte = np.where(mant > 0.5, ex, ex - 1) + 127
    byte = np.clip(np.where(amax > 0, byte, 1), 1, 254)
    scaled = (w * np.exp2(127.0 - byte)[:, None, :]).reshape(k, n).astype(np.float32)
    by_word = np.ascontiguousarray(scaled.reshape(k // 512, 128, 4, n).transpose(0, 1, 3, 2))
    if fmt == "e4m3":
        words = by_word.astype(ml_dtypes.float8_e4m3fn).view(np.uint8)
    else:
        c = by_word.astype(ml_dtypes.float4_e2m1fn).view(np.uint8) & 0xF
        words = (c[..., 0::2] | (c[..., 1::2] << 4)).reshape(k // 512, 128, 2 * n)
    return np.ascontiguousarray(words), np.ascontiguousarray(byte.astype(np.uint8).reshape(k // 512, 16, n))


def unpack_weight(words, scales, fmt):
    g, _, n = scales.shape
    words = np.ascontiguousarray(words).reshape(g, 128, n, -1)
    if fmt == "e4m3":
        vals = words.view(ml_dtypes.float8_e4m3fn).astype(np.float64)
    else:
        nib = np.empty((g, 128, n, 4), np.uint8)
        nib[..., 0::2] = words & 0xF
        nib[..., 1::2] = words >> 4
        vals = E2M1[nib]
    vals = vals * np.repeat(np.exp2(scales.astype(np.float64) - 127.0), 8, axis=1)[..., None]
    return vals.transpose(0, 1, 3, 2).reshape(g * 512, n)


D, T, U, I, Q = 512, 1024, 1024, 512, 128


def setup_inputs():
    n = np.random.standard_normal
    idx = np.stack([np.random.permutation(T)[:I] for _ in range(8)])
    idx2 = np.stack([np.random.permutation(I)[:I] for _ in range(8)])
    idx3 = np.stack([np.random.permutation(T)[:I] for _ in range(8)])
    idx4 = np.stack([np.random.permutation(U)[:I] for _ in range(8)])
    idx5 = np.stack([np.random.permutation(T)[:I] for _ in range(8)])
    idx6 = np.stack([np.random.permutation(U)[:I] for _ in range(8)])
    fd = mx_kscale(D)
    keysp = pack_weight(n((D, T)) / fd[:, None], "e4m3")
    notesp = pack_weight(n((D, U)) / fd[:, None], "e2m1")
    return {
        "query": (n((D, Q)) * 1.0 / np.sqrt(D) * fd[:, None]).astype(np.float32),
        "keys_words": keysp[0],
        "keys_scales": keysp[1],
        "notes_words": notesp[0],
        "notes_scales": notesp[1],
        "offs": striped8(idx),
        "offs2": striped8(idx2),
        "offs3": striped8(idx3),
        "offs4": striped8(idx4),
        "offs5": striped8(idx5),
        "offs6": striped8(idx6),
    }


def reference(query, keys_words, keys_scales, notes_words, notes_scales, offs, offs2, offs3, offs4, offs5, offs6):
    idx = unstriped8(offs)
    idx2 = unstriped8(offs2)
    idx3 = unstriped8(offs3)
    idx4 = unstriped8(offs4)
    idx5 = unstriped8(offs5)
    idx6 = unstriped8(offs6)
    keysu = unpack_weight(keys_words, keys_scales, "e4m3")
    notesu = unpack_weight(notes_words, notes_scales, "e2m1")
    queryq = mxq(f64(query), 0, "e4m3")
    a = queryq.T @ keysu
    b = queryq.T @ notesu
    w = pick8(a, idx, 16) * 1.25
    v = pick8(w, idx2, 16)
    f1 = np.zeros((Q, T))
    f1[np.arange(Q)[:, None], idx3[np.arange(Q) % 128 // 16]] = v
    f2 = np.zeros((Q, U))
    f2[np.arange(Q)[:, None], idx4[np.arange(Q) % 128 // 16]] = w
    aa = a + f1
    bb = b - f2
    y = pick8(aa, idx5, 16) - pick8(bb, idx6, 16)
    return y

@@ -1,0 +1,138 @@
+from contextlib import ExitStack
+
+import concourse.mybir as mybir
+
+D, T, U, I, Q = 512, 1024, 1024, 512, 128
+FLOPS = 2 * D * Q * (T + U)
+
+F32 = mybir.dt.float32
+BF16 = mybir.dt.bfloat16
+I32 = mybir.dt.int32
+U32 = mybir.dt.uint32
+U16 = mybir.dt.uint16
+U8 = mybir.dt.uint8
+FP8X4 = mybir.dt.float8_e4m3fn_x4
+FP4X4 = mybir.dt.float4_e2m1fn_x4
+MULT = mybir.AluOpType.mult
+ADD = mybir.AluOpType.add
+SUB = mybir.AluOpType.subtract
+COPY = mybir.ActivationFunctionType.Copy
+
+P = 128
+PACK = 4
+BANK = 512
+HALF = I // 2
+LIST_COLS = I // 16
+Q_SCALAR = 64
+AA_V = 704
+
+
+def tile_attend_slotchain_two_kernel(tc, query, keys_words, keys_scales, notes_words, notes_scales,
+                                      offs, offs2, offs3, offs4, offs5, offs6, out):
+    nc = tc.nc
+    with ExitStack() as ctx:
+        sb = ctx.enter_context(tc.tile_pool(name="sb", bufs=1))
+        ps = ctx.enter_context(tc.psum_pool(name="ps", bufs=1))
+
+        k_scale = sb.tile([P, T], U8, name="k_scale", align_bytes=64)
+        n_scale = sb.tile([P, U], U8, name="n_scale", align_bytes=64)
+        f1 = sb.tile([P, T], F32, name="f1")
+        f2 = sb.tile([P, U], F32, name="f2")
+        nc.vector.memset(k_scale[:].bitcast(U32), 0)
+        nc.vector.memset(n_scale[:].bitcast(U32), 0)
+        nc.vector.memset(f2[:].bitcast(U32), 0)
+        nc.vector.memset(f1[:].bitcast(U32), 0)
+
+        def load_list(src, name):
+            t = sb.tile([P, LIST_COLS], U16, name=name)
+            nc.sync.dma_start(t[:], src)
+            return t
+
+        def load_scales(plane, src):
+            for quad in range(4):
+                nc.sync.dma_start(plane[32 * quad:32 * quad + 4, :].bitcast(I32),
+                                  src[0, 4 * quad:4 * quad + 4, :].bitcast(I32))
+
+        q_raw = sb.tile([P, PACK, Q], F32, name="q_raw")
+        nc.sync.dma_start(q_raw[:], query.rearrange("(p j) w -> p j w", j=PACK))
+        load_scales(k_scale, keys_scales)
+        k_src = keys_words[0].rearrange("p n t -> p (n t)").bitcast(I32)
+        k_words = []
+        for h in range(2):
+            kw = sb.tile([P, BANK], I32, name="k_words%d" % h, align_bytes=64)
+            nc.sync.dma_start(kw[:], k_src[:, h * BANK:(h + 1) * BANK])
+            k_words.append(kw)
+        l1 = load_list(offs, "l1")
+        l4 = load_list(offs4, "l4")
+        l2 = load_list(offs2, "l2")
+        l3 = load_list(offs3, "l3")
+        n_words = sb.tile([P, 2 * U], U8, name="n_words", align_bytes=64)
+        nc.sync.dma_start(n_words[:].bitcast(I32), notes_words[0].bitcast(I32))
+        load_scales(n_scale, notes_scales)
+        l6 = load_list(offs6, "l6")
+        l5 = load_list(offs5, "l5")
+
+        q_bf = sb.tile([P, Q, PACK], BF16, name="q_bf", align_bytes=64)
+        q_view = q_raw[:].rearrange("p j w -> p w j")
+        nc.scalar.copy(q_bf[:, :Q_SCALAR, :], q_view[:, :Q_SCALAR, :])
+        nc.vector.tensor_copy(q_bf[:, Q_SCALAR:, :], q_view[:, Q_SCALAR:, :])
+        q_codes = sb.tile([P, Q], U32, name="q_codes", align_bytes=64)
+        q_scale = sb.tile([P, Q], U8, name="q_scale", align_bytes=64)
+        nc.vector.quantize_mx(out=q_codes[:].bitcast(FP8X4), scales=q_scale[:],
+                              in_=q_bf[:].rearrange("p w j -> p (w j)"))
+
+        a_sb = sb.tile([P, T], F32, name="a_sb")
+        parts = [(0, 512), (512, 256), (768, 256)]
+        a_ps = []
+        for n, (c0, width) in enumerate(parts):
+            bank = ps.tile([P, width], F32, name="a_ps%d" % n)
+            kw = k_words[c0 // BANK]
+            nc.tensor.matmul_mx(out=bank[:], lhsT=q_codes[:].bitcast(FP8X4), lhsT_scale=q_scale[:],
+                                rhs=kw[:, c0 % BANK:c0 % BANK + width].bitcast(FP8X4),
+                                rhs_scale=k_scale[:, c0:c0 + width], start=True, stop=True)
+            a_ps.append(bank)
+        nc.vector.tensor_copy(a_sb[:, 0:512], a_ps[0][:])
+        nc.scalar.copy(a_sb[:, 512:768], a_ps[1][:])
+        nc.scalar.copy(a_sb[:, 768:1024], a_ps[2][:])
+
+        b_ps = []
+        for h in range(2):
+            bank = ps.tile([P, BANK], F32, name="b_ps%d" % h)
+            nc.tensor.matmul_mx(out=bank[:], lhsT=q_codes[:].bitcast(FP8X4), lhsT_scale=q_scale[:],
+                                rhs=n_words[:, 2 * h * BANK:2 * (h + 1) * BANK].bitcast(FP4X4),
+                                rhs_scale=n_scale[:, h * BANK:(h + 1) * BANK], start=True, stop=True)
+            b_ps.append(bank)
+
+        lo = slice(0, LIST_COLS // 2)
+        hi = slice(LIST_COLS // 2, LIST_COLS)
+        w = sb.tile([P, I], F32, name="w")
+        nc.vector.tensor_scalar(w[:, :HALF], a_sb[:].indirect(l1[:, lo]), 1.25, 0.0, MULT, ADD)
+        nc.scalar.activation(w[:, HALF:], a_sb[:].indirect(l1[:, hi]), COPY, scale=1.25)
+
+        nc.vector.tensor_copy(f2[:].indirect(l4[:]), w[:])
+        v = sb.tile([P, I], F32, name="v")
+        nc.scalar.activation(v[:, :HALF], w[:].indirect(l2[:, lo]), COPY)
+        nc.scalar.activation(v[:, HALF:], w[:].indirect(l2[:, hi]), COPY)
+
+        b_sb = sb.tile([P, U], F32, name="b_sb", tag="b_then_aa")
+        for h in range(2):
+            nc.scalar.copy(b_sb[:, h * BANK:(h + 1) * BANK], b_ps[h][:])
+        bb = sb.tile([P, U], F32, name="bb")
+        nc.gpsimd.tensor_tensor(bb[:], b_sb[:], f2[:], SUB)
+        nc.vector.tensor_copy(f1[:].indirect(l3[:]), v[:])
+        gb = sb.tile([P, I], F32, name="gb")
+        nc.scalar.activation(gb[:], bb[:].indirect(l6[:]), COPY)
+
+        aa = sb.tile([P, T], F32, name="aa", tag="b_then_aa")
+        nc.gpsimd.tensor_tensor(aa[:, AA_V:], a_sb[:, AA_V:], f1[:, AA_V:], ADD)
+        nc.vector.tensor_tensor(aa[:, :BANK], a_ps[0][:], f1[:, :BANK], ADD)
+        nc.vector.tensor_tensor(aa[:, BANK:AA_V], a_ps[1][:, :AA_V - BANK], f1[:, BANK:AA_V], ADD)
+
+        y_lo = sb.tile([P, HALF], F32, name="y_lo")
+        y_hi = sb.tile([P, HALF], F32, name="y_hi")
+        ga = sb.tile([P, HALF], F32, name="ga")
+        nc.vector.tensor_tensor(y_lo[:], aa[:].indirect(l5[:, lo]), gb[:, :HALF], SUB)
+        nc.scalar.activation(ga[:], aa[:].indirect(l5[:, hi]), COPY)
+        nc.sync.dma_start(out[:, :HALF], y_lo[:])
+        nc.vector.tensor_tensor(y_hi[:], ga[:], gb[:, HALF:], SUB)
+        nc.sync.dma_start(out[:, HALF:], y_hi[:])

@@ -23,7 +23,7 @@ PACK = 4
 BANK = 512
 HALF = I // 2
 LIST_COLS = I // 16
-Q_SCALAR = 64
+Q_SCALAR = 48
 AA_V = 704
 
 
@@ -34,14 +34,12 @@ def tile_attend_slotchain_two_kernel(tc, query, keys_words, keys_scales, notes_w
         sb = ctx.enter_context(tc.tile_pool(name="sb", bufs=1))
         ps = ctx.enter_context(tc.psum_pool(name="ps", bufs=1))
 
-        k_scale = sb.tile([P, T], U8, name="k_scale", align_bytes=64)
+        k_scale = sb.tile([P, T // 4], U8, name="k_scale", align_bytes=64)
         n_scale = sb.tile([P, U], U8, name="n_scale", align_bytes=64)
-        f1 = sb.tile([P, T], F32, name="f1")
         f2 = sb.tile([P, U], F32, name="f2")
         nc.vector.memset(k_scale[:].bitcast(U32), 0)
         nc.vector.memset(n_scale[:].bitcast(U32), 0)
         nc.vector.memset(f2[:].bitcast(U32), 0)
-        nc.vector.memset(f1[:].bitcast(U32), 0)
 
         def load_list(src, name):
             t = sb.tile([P, LIST_COLS], U16, name=name)
@@ -55,24 +53,28 @@ def tile_attend_slotchain_two_kernel(tc, query, keys_words, keys_scales, notes_w
 
         q_raw = sb.tile([P, PACK, Q], F32, name="q_raw")
         nc.sync.dma_start(q_raw[:], query.rearrange("(p j) w -> p j w", j=PACK))
-        load_scales(k_scale, keys_scales)
         k_src = keys_words[0].rearrange("p n t -> p (n t)").bitcast(I32)
         k_words = []
         for h in range(2):
             kw = sb.tile([P, BANK], I32, name="k_words%d" % h, align_bytes=64)
             nc.sync.dma_start(kw[:], k_src[:, h * BANK:(h + 1) * BANK])
             k_words.append(kw)
+            if h == 0:
+                for quad in range(4):
+                    rows = keys_scales[0, 4 * quad:4 * quad + 4, :].bitcast(I32)
+                    nc.sync.dma_start(k_scale[32 * quad:32 * quad + 16, :].bitcast(I32),
+                                      rows.rearrange("r (j c) -> j r c", j=4))
         l1 = load_list(offs, "l1")
         l4 = load_list(offs4, "l4")
-        l2 = load_list(offs2, "l2")
-        l3 = load_list(offs3, "l3")
         n_words = sb.tile([P, 2 * U], U8, name="n_words", align_bytes=64)
         nc.sync.dma_start(n_words[:].bitcast(I32), notes_words[0].bitcast(I32))
         load_scales(n_scale, notes_scales)
+        l2 = load_list(offs2, "l2")
+        l3 = load_list(offs3, "l3")
         l6 = load_list(offs6, "l6")
         l5 = load_list(offs5, "l5")
 
-        q_bf = sb.tile([P, Q, PACK], BF16, name="q_bf", align_bytes=64)
+        q_bf = sb.tile([P, Q, PACK], BF16, name="q_bf", tag="q_then_f1", align_bytes=64)
         q_view = q_raw[:].rearrange("p j w -> p w j")
         nc.scalar.copy(q_bf[:, :Q_SCALAR, :], q_view[:, :Q_SCALAR, :])
         nc.vector.tensor_copy(q_bf[:, Q_SCALAR:, :], q_view[:, Q_SCALAR:, :])
@@ -82,15 +84,12 @@ def tile_attend_slotchain_two_kernel(tc, query, keys_words, keys_scales, notes_w
                               in_=q_bf[:].rearrange("p w j -> p (w j)"))
 
         a_sb = sb.tile([P, T], F32, name="a_sb")
-        parts = [(0, 512), (512, 256), (768, 256)]
-        a_ps = []
-        for n, (c0, width) in enumerate(parts):
-            bank = ps.tile([P, width], F32, name="a_ps%d" % n)
-            kw = k_words[c0 // BANK]
-            nc.tensor.matmul_mx(out=bank[:], lhsT=q_codes[:].bitcast(FP8X4), lhsT_scale=q_scale[:],
-                                rhs=kw[:, c0 % BANK:c0 % BANK + width].bitcast(FP8X4),
-                                rhs_scale=k_scale[:, c0:c0 + width], start=True, stop=True)
-            a_ps.append(bank)
+        a_ps = [ps.tile([P, width], F32, name="a_ps%d" % n) for n, width in enumerate((512, 256, 256))]
+        outs = [a_ps[0][:, :256], a_ps[0][:, 256:], a_ps[1][:], a_ps[2][:]]
+        for j in range(4):
+            nc.tensor.matmul_mx(out=outs[j], lhsT=q_codes[:].bitcast(FP8X4), lhsT_scale=q_scale[:],
+                                rhs=k_words[j // 2][:, (j % 2) * 256:(j % 2 + 1) * 256].bitcast(FP8X4),
+                                rhs_scale=k_scale[4 * j:, :], start=True, stop=True)
         nc.vector.tensor_copy(a_sb[:, 0:512], a_ps[0][:])
         nc.scalar.copy(a_sb[:, 512:768], a_ps[1][:])
         nc.scalar.copy(a_sb[:, 768:1024], a_ps[2][:])
@@ -102,6 +101,9 @@ def tile_attend_slotchain_two_kernel(tc, query, keys_words, keys_scales, notes_w
                                 rhs=n_words[:, 2 * h * BANK:2 * (h + 1) * BANK].bitcast(FP4X4),
                                 rhs_scale=n_scale[:, h * BANK:(h + 1) * BANK], start=True, stop=True)
             b_ps.append(bank)
+
+        f1 = sb.tile([P, T], F32, name="f1", tag="q_then_f1", align_bytes=64)
+        nc.gpsimd.memset(f1[:], 0.0)
 
         lo = slice(0, LIST_COLS // 2)
         hi = slice(LIST_COLS // 2, LIST_COLS)

from contextlib import ExitStack

import concourse.mybir as mybir

D, T, U, I, Q = 512, 1024, 1024, 512, 128
FLOPS = 2 * D * Q * (T + U)

F32 = mybir.dt.float32
BF16 = mybir.dt.bfloat16
I32 = mybir.dt.int32
U32 = mybir.dt.uint32
U16 = mybir.dt.uint16
U8 = mybir.dt.uint8
FP8X4 = mybir.dt.float8_e4m3fn_x4
FP4X4 = mybir.dt.float4_e2m1fn_x4
MULT = mybir.AluOpType.mult
ADD = mybir.AluOpType.add
SUB = mybir.AluOpType.subtract
COPY = mybir.ActivationFunctionType.Copy

P = 128
PACK = 4
BANK = 512
HALF = I // 2
LIST_COLS = I // 16
Q_SCALAR = 48
AA_V = 704


def tile_attend_slotchain_two_kernel(tc, query, keys_words, keys_scales, notes_words, notes_scales,
                                      offs, offs2, offs3, offs4, offs5, offs6, out):
    nc = tc.nc
    with ExitStack() as ctx:
        sb = ctx.enter_context(tc.tile_pool(name="sb", bufs=1))
        ps = ctx.enter_context(tc.psum_pool(name="ps", bufs=1))

        k_scale = sb.tile([P, T // 4], U8, name="k_scale", align_bytes=64)
        n_scale = sb.tile([P, U], U8, name="n_scale", align_bytes=64)
        f2 = sb.tile([P, U], F32, name="f2")
        nc.vector.memset(k_scale[:].bitcast(U32), 0)
        nc.vector.memset(n_scale[:].bitcast(U32), 0)
        nc.vector.memset(f2[:].bitcast(U32), 0)

        def load_list(src, name):
            t = sb.tile([P, LIST_COLS], U16, name=name)
            nc.sync.dma_start(t[:], src)
            return t

        def load_scales(plane, src):
            for quad in range(4):
                nc.sync.dma_start(plane[32 * quad:32 * quad + 4, :].bitcast(I32),
                                  src[0, 4 * quad:4 * quad + 4, :].bitcast(I32))

        q_raw = sb.tile([P, PACK, Q], F32, name="q_raw")
        nc.sync.dma_start(q_raw[:], query.rearrange("(p j) w -> p j w", j=PACK))
        k_src = keys_words[0].rearrange("p n t -> p (n t)").bitcast(I32)
        k_words = []
        for h in range(2):
            kw = sb.tile([P, BANK], I32, name="k_words%d" % h, align_bytes=64)
            nc.sync.dma_start(kw[:], k_src[:, h * BANK:(h + 1) * BANK])
            k_words.append(kw)
            if h == 0:
                for quad in range(4):
                    rows = keys_scales[0, 4 * quad:4 * quad + 4, :].bitcast(I32)
                    nc.sync.dma_start(k_scale[32 * quad:32 * quad + 16, :].bitcast(I32),
                                      rows.rearrange("r (j c) -> j r c", j=4))
        l1 = load_list(offs, "l1")
        l4 = load_list(offs4, "l4")
        n_words = sb.tile([P, 2 * U], U8, name="n_words", align_bytes=64)
        nc.sync.dma_start(n_words[:].bitcast(I32), notes_words[0].bitcast(I32))
        load_scales(n_scale, notes_scales)
        l2 = load_list(offs2, "l2")
        l3 = load_list(offs3, "l3")
        l6 = load_list(offs6, "l6")
        l5 = load_list(offs5, "l5")

        q_bf = sb.tile([P, Q, PACK], BF16, name="q_bf", tag="q_then_f1", align_bytes=64)
        q_view = q_raw[:].rearrange("p j w -> p w j")
        nc.scalar.copy(q_bf[:, :Q_SCALAR, :], q_view[:, :Q_SCALAR, :])
        nc.vector.tensor_copy(q_bf[:, Q_SCALAR:, :], q_view[:, Q_SCALAR:, :])
        q_codes = sb.tile([P, Q], U32, name="q_codes", align_bytes=64)
        q_scale = sb.tile([P, Q], U8, name="q_scale", align_bytes=64)
        nc.vector.quantize_mx(out=q_codes[:].bitcast(FP8X4), scales=q_scale[:],
                              in_=q_bf[:].rearrange("p w j -> p (w j)"))

        a_sb = sb.tile([P, T], F32, name="a_sb")
        a_ps = [ps.tile([P, width], F32, name="a_ps%d" % n) for n, width in enumerate((512, 256, 256))]
        outs = [a_ps[0][:, :256], a_ps[0][:, 256:], a_ps[1][:], a_ps[2][:]]
        for j in range(4):
            nc.tensor.matmul_mx(out=outs[j], lhsT=q_codes[:].bitcast(FP8X4), lhsT_scale=q_scale[:],
                                rhs=k_words[j // 2][:, (j % 2) * 256:(j % 2 + 1) * 256].bitcast(FP8X4),
                                rhs_scale=k_scale[4 * j:, :], start=True, stop=True)
        nc.vector.tensor_copy(a_sb[:, 0:512], a_ps[0][:])
        nc.scalar.copy(a_sb[:, 512:768], a_ps[1][:])
        nc.scalar.copy(a_sb[:, 768:1024], a_ps[2][:])

        b_ps = []
        for h in range(2):
            bank = ps.tile([P, BANK], F32, name="b_ps%d" % h)
            nc.tensor.matmul_mx(out=bank[:], lhsT=q_codes[:].bitcast(FP8X4), lhsT_scale=q_scale[:],
                                rhs=n_words[:, 2 * h * BANK:2 * (h + 1) * BANK].bitcast(FP4X4),
                                rhs_scale=n_scale[:, h * BANK:(h + 1) * BANK], start=True, stop=True)
            b_ps.append(bank)

        f1 = sb.tile([P, T], F32, name="f1", tag="q_then_f1", align_bytes=64)
        nc.gpsimd.memset(f1[:], 0.0)

        lo = slice(0, LIST_COLS // 2)
        hi = slice(LIST_COLS // 2, LIST_COLS)
        w = sb.tile([P, I], F32, name="w")
        nc.vector.tensor_scalar(w[:, :HALF], a_sb[:].indirect(l1[:, lo]), 1.25, 0.0, MULT, ADD)
        nc.scalar.activation(w[:, HALF:], a_sb[:].indirect(l1[:, hi]), COPY, scale=1.25)

        nc.vector.tensor_copy(f2[:].indirect(l4[:]), w[:])
        v = sb.tile([P, I], F32, name="v")
        nc.scalar.activation(v[:, :HALF], w[:].indirect(l2[:, lo]), COPY)
        nc.scalar.activation(v[:, HALF:], w[:].indirect(l2[:, hi]), COPY)

        b_sb = sb.tile([P, U], F32, name="b_sb", tag="b_then_aa")
        for h in range(2):
            nc.scalar.copy(b_sb[:, h * BANK:(h + 1) * BANK], b_ps[h][:])
        bb = sb.tile([P, U], F32, name="bb")
        nc.gpsimd.tensor_tensor(bb[:], b_sb[:], f2[:], SUB)
        nc.vector.tensor_copy(f1[:].indirect(l3[:]), v[:])
        gb = sb.tile([P, I], F32, name="gb")
        nc.scalar.activation(gb[:], bb[:].indirect(l6[:]), COPY)

        aa = sb.tile([P, T], F32, name="aa", tag="b_then_aa")
        nc.gpsimd.tensor_tensor(aa[:, AA_V:], a_sb[:, AA_V:], f1[:, AA_V:], ADD)
        nc.vector.tensor_tensor(aa[:, :BANK], a_ps[0][:], f1[:, :BANK], ADD)
        nc.vector.tensor_tensor(aa[:, BANK:AA_V], a_ps[1][:, :AA_V - BANK], f1[:, BANK:AA_V], ADD)

        y_lo = sb.tile([P, HALF], F32, name="y_lo")
        y_hi = sb.tile([P, HALF], F32, name="y_hi")
        ga = sb.tile([P, HALF], F32, name="ga")
        nc.vector.tensor_tensor(y_lo[:], aa[:].indirect(l5[:, lo]), gb[:, :HALF], SUB)
        nc.scalar.activation(ga[:], aa[:].indirect(l5[:, hi]), COPY)
        nc.sync.dma_start(out[:, :HALF], y_lo[:])
        nc.vector.tensor_tensor(y_hi[:], ga[:], gb[:, HALF:], SUB)
        nc.sync.dma_start(out[:, HALF:], y_hi[:])
